import numpy as np
import ml_dtypes


def mxq(x, axis, fmt="e4m3"):
    dtype, down = {"e4m3": (ml_dtypes.float8_e4m3fn, 7), "e5m2": (ml_dtypes.float8_e5m2, 14)}[fmt]
    v = np.moveaxis(np.asarray(x, np.float32).astype(ml_dtypes.bfloat16).astype(np.float64), axis, -1)
    blocks = v.reshape(v.shape[:-1] + (-1, 32))
    amax = np.abs(blocks).max(-1, keepdims=True)
    byte = np.maximum(np.where(amax > 0, np.frexp(amax)[1] - 1 + 127, 0) - down, 1)
    scale = np.exp2(byte - 127.0)
    codes = (blocks / scale).astype(np.float32).astype(dtype).astype(np.float64)
    return np.moveaxis((codes * scale).reshape(v.shape), -1, axis)


WIDE = False


def mx_kscale(k):
    if not WIDE:
        return np.ones(k)
    levels = np.array([10, -10, 5, -5, 0])
    if k % 512:
        return np.exp2(np.random.permutation(np.resize(levels, k // 32))).repeat(32)
    a = np.empty((k // 512, 16))
    for p in range(k // 512):
        a[p, :8] = np.random.permutation(np.resize(levels, 8))
        for g in range(8):
            far = levels[np.abs(levels - a[p, g]) >= 10]
            a[p, g + 8] = far[np.random.randint(len(far))]
    return np.exp2(a.ravel()).repeat(32)


def f64(x):
    return np.asarray(x).astype(np.float64)


def striped(idx):
    return np.tile(idx.reshape(-1, 16).T, (8, 1)).astype(np.uint16)


def unstriped(offs):
    return offs[:16].T.reshape(-1).astype(np.int64)


def striped8(idx):
    return np.concatenate([x.reshape(-1, 16).T for x in idx]).astype(np.uint16)


def runs(offs, k):
    lists = np.stack([offs[16 * r : 16 * r + 16].T.reshape(-1) for r in range(8)]).astype(np.int64)
    return lists[np.arange(k) % 512 // 64]


def pack_weight(w):
    k, n = w.shape
    w = f64(np.asarray(w, np.float32).astype(ml_dtypes.bfloat16)).reshape(k // 32, 32, n)
    amax = np.abs(w).max(1)
    byte = np.clip(np.where(amax > 0, np.frexp(amax)[1] - 1 + 127 - 7, 1), 1, 254)
    scaled = (w * np.exp2(127.0 - byte)[:, None, :]).reshape(k, n).astype(np.float32)
    words = np.ascontiguousarray(scaled.reshape(k // 512, 128, 4, n).transpose(0, 1, 3, 2)).astype(ml_dtypes.float8_e4m3fn).view(np.uint8)
    return words, np.ascontiguousarray(byte.astype(np.uint8).reshape(k // 512, 16, n))


def unpack_weight(words, scales):
    g, p, n, _ = words.shape
    vals = np.ascontiguousarray(words).view(ml_dtypes.float8_e4m3fn).astype(np.float64) * np.repeat(np.exp2(scales.astype(np.float64) - 127.0), 8, axis=1)[..., None]
    return vals.transpose(0, 1, 3, 2).reshape(g * 512, n)


K, T, S, V, N, H = 512, 2048, 512, 256, 512, 512


def setup_inputs():
    n = np.random.standard_normal
    s = mx_kscale(K)[:, None]
    u = mx_kscale(H)
    packed_xT = pack_weight(n((K, T)) * s)
    perm = np.stack([np.random.permutation(S) for _ in range(8)])
    perm2 = np.stack([np.random.permutation(S) for _ in range(8)])
    return {
        "x_words": packed_xT[0],
        "x_scales": packed_xT[1],
        "w1": (n((K, H)) / np.sqrt(K) / s).astype(np.float32),
        "gn": (np.random.uniform(0.5, 1.5, (H, 1)) * u[:, None]).astype(np.float32),
        "w2": (n((H, N)) / np.sqrt(H) / u[:, None]).astype(np.float32),
        "offs": striped(np.random.permutation(T)[:S]),
        "la": striped8(perm[:, :V]),
        "lb": striped8(perm[:, V:]),
        "ma": striped8(perm2[:, :V]),
        "mb": striped8(perm2[:, V:]),
    }


def reference(x_words, x_scales, w1, gn, w2, offs, la, lb, ma, mb):
    xq = unpack_weight(x_words, x_scales)[:, unstriped(offs)]
    y = mxq(f64(w1), 0, "e4m3").T @ xq
    m1 = 0.5 * (y[np.arange(H)[:, None], runs(la, H)] + y[np.arange(H)[:, None], runs(lb, H)])
    m0 = y[np.arange(H)[:, None], runs(lb, H)] - (0.5 * m1)
    h0 = np.zeros((H, S))
    h0[np.arange(H)[:, None], runs(lb, H)] = m0
    h = h0.copy()
    h[np.arange(H)[:, None], runs(la, H)] = m1
    m3 = np.minimum(h[np.arange(H)[:, None], runs(ma, H)], h[np.arange(H)[:, None], runs(mb, H)])
    m2 = np.maximum(h[np.arange(H)[:, None], runs(ma, H)], h[np.arange(H)[:, None], runs(mb, H)])
    h2 = np.zeros((H, S))
    h2[np.arange(H)[:, None], runs(ma, H)] = m2
    h3 = h2.copy()
    h3[np.arange(H)[:, None], runs(mb, H)] = m3
    z = f64(gn) * h3
    return mxq(f64(w2), 0, "e4m3").T @ mxq(z, 0, "e4m3")

@@ -1,0 +1,172 @@
+from contextlib import ExitStack
+
+import concourse.mybir as mybir
+
+K, T, S, V, N, H = 512, 2048, 512, 256, 512, 512
+FLOPS = 2 * K * H * S + 2 * H * N * S
+
+F32 = mybir.dt.float32
+BF16 = mybir.dt.bfloat16
+I32 = mybir.dt.int32
+U32 = mybir.dt.uint32
+U16 = mybir.dt.uint16
+U8 = mybir.dt.uint8
+FP8X4 = mybir.dt.float8_e4m3fn_x4
+ALU = mybir.AluOpType
+ACT = mybir.ActivationFunctionType
+
+P = 128
+PACK = 4
+HALF = S // 2
+W1_SPLIT = 40
+ORDER = (0, 2, 3, 1)
+
+
+def tile_picked_gossip2_none_p_kernel(tc, x_words, x_scales, w1, gn, w2, offs, la, lb, ma, mb, out):
+    nc = tc.nc
+    with ExitStack() as ctx:
+        keep = ctx.enter_context(tc.tile_pool(name="keep", bufs=1))
+        ring = ctx.enter_context(tc.tile_pool(name="ring", bufs=3))
+        psum = ctx.enter_context(tc.psum_pool(name="psum", bufs=8))
+
+        offs_t = keep.tile([P, S // 16], U16, name="offs_t")
+        la_t = keep.tile([P, V // 16], U16, name="la_t")
+        lb_t = keep.tile([P, V // 16], U16, name="lb_t")
+        ma_t = keep.tile([P, V // 16], U16, name="ma_t")
+        mb_t = keep.tile([P, V // 16], U16, name="mb_t")
+
+        xs_all = keep.tile([P, T], U8, name="xs_all")
+        nc.gpsimd.memset(xs_all[:].bitcast(I32), 0)
+        for q in range(4):
+            nc.scalar.dma_start(out=xs_all[32 * q : 32 * q + 4, :].bitcast(I32), in_=x_scales[0][4 * q : 4 * q + 4, :].bitcast(I32))
+
+        for list_tile, src_list in ((offs_t, offs), (la_t, la), (lb_t, lb), (ma_t, ma)):
+            nc.sync.dma_start(out=list_tile[:], in_=src_list)
+        xw_all = keep.tile([P, T], U32, name="xw_all")
+        nc.sync.dma_start(out=xw_all[:].bitcast(I32), in_=x_words[0].rearrange("p n t -> p (n t)").bitcast(I32))
+        w1_rows = w1.rearrange("(p j) c -> p j c", j=PACK)
+        w1_raw = []
+        for half, tag in enumerate(("w1_raw", "w_raw")):
+            raw = keep.tile([P, PACK, H // 2], F32, name=tag)
+            nc.sync.dma_start(out=raw[:], in_=w1_rows[:, :, half * (H // 2) : (half + 1) * (H // 2)])
+            w1_raw.append(raw[:].rearrange("p j (m t) -> p m j t", t=PACK))
+        nc.sync.dma_start(out=mb_t[:], in_=mb)
+
+        xw = keep.tile([P, S], U32, name="xw", align_bytes=64)
+        nc.vector.tensor_copy(xw[:], xw_all[:].indirect(offs_t[:]))
+        xs = keep.tile([P, S], U8, name="xs", align_bytes=64)
+        nc.vector.tensor_copy(xs[:], xs_all[:].indirect(offs_t[:]))
+
+        w1_bf = keep.tile([P, PACK * H], BF16, name="w1_bf", align_bytes=64)
+        dst = w1_bf[:].rearrange("p (t m j) -> p m j t", t=PACK, j=PACK)
+        nc.scalar.copy(dst[:, :64], w1_raw[0])
+        nc.vector.tensor_copy(dst[:, 64 : 64 + W1_SPLIT], w1_raw[1][:, :W1_SPLIT])
+        nc.scalar.copy(dst[:, 64 + W1_SPLIT :], w1_raw[1][:, W1_SPLIT:])
+        w1_codes = keep.tile([P, H], U32, name="w1_codes", align_bytes=64)
+        w1_scales = keep.tile([P, H], U8, name="w1_scales", align_bytes=64)
+        for c0, c1 in ((0, P), (2 * P, 4 * P), (P, 2 * P)):
+            nc.vector.quantize_mx(out=w1_codes[:, c0:c1].bitcast(FP8X4), scales=w1_scales[:, c0:c1], in_=w1_bf[:, PACK * c0 : PACK * c1])
+
+        w2_raw = keep.tile([P, PACK, N], F32, name="w_raw")
+        nc.sync.dma_start(out=w2_raw[:], in_=w2.rearrange("(p j) c -> p j c", j=PACK))
+
+        gain = keep.tile([P, PACK], F32, name="xs_all")
+        nc.sync.dma_start(out=gain[:], in_=gn.rearrange("(p t) o -> p (t o)", t=PACK))
+        y = [keep.tile([P, S], F32, name=f"y{t}") for t in range(PACK)]
+        for t in ORDER:
+            cols = slice(t * P, (t + 1) * P)
+            for c0, c1 in ((0, HALF), (HALF, S)) if t == 0 else ((0, S),):
+                acc = psum.tile([P, S], F32, name="acc")
+                nc.tensor.matmul_mx(
+                    out=acc[:, : c1 - c0],
+                    lhsT=w1_codes[:, cols].bitcast(FP8X4),
+                    lhsT_scale=w1_scales[:, cols],
+                    rhs=xw[:, c0:c1].bitcast(FP8X4),
+                    rhs_scale=xs[:, c0:c1],
+                    start=True,
+                    stop=True,
+                )
+                nc.scalar.activation(y[t][:, c0:c1], acc[:, : c1 - c0], ACT.Copy, scale=0.5)
+
+        def small(name):
+            return [keep.tile([P, V], F32, name=f"{name}{t}") for t in range(PACK)]
+
+        a, b, a2, b2 = small("a"), small("b"), small("a2"), small("b2")
+        c, e, up, dn0, dn = small("c"), small("e"), small("up"), small("dn0"), small("dn")
+        h = [keep.tile([P, S], F32, name=f"h{t}") for t in range(PACK)]
+        h3 = {}
+
+        for t in ORDER:
+            nc.vector.tensor_copy(a[t][:], y[t][:].indirect(la_t[:]))
+            nc.vector.tensor_copy(b[t][:], y[t][:].indirect(lb_t[:]))
+            nc.scalar.activation(a2[t][:], a[t][:], ACT.Copy, scale=-0.5)
+            nc.scalar.activation(b2[t][:], b[t][:], ACT.Copy, scale=1.5)
+        for t in ORDER:
+            nc.vector.tensor_tensor(h[t][:].indirect(la_t[:]), a[t][:], b[t][:], ALU.add)
+
+        w2_bf = keep.tile([P, PACK * N], BF16, name="w2_bf", align_bytes=64)
+        dst2 = w2_bf[:].rearrange("p (c i j) -> p c j i", i=4, j=PACK)
+        src2 = w2_raw[:].rearrange("p j (c i) -> p c j i", i=4)
+        for mt in range(4):
+            nc.scalar.copy(dst2[:, 32 * mt : 32 * (mt + 1)], src2[:, 32 * mt : 32 * (mt + 1)])
+
+        for t in ORDER:
+            nc.vector.tensor_tensor(h[t][:].indirect(lb_t[:]), a2[t][:], b2[t][:], ALU.add)
+        for t in ORDER:
+            nc.vector.tensor_copy(c[t][:], h[t][:].indirect(ma_t[:]))
+        w2_codes = keep.tile([P, N], U32, name="w2_codes", align_bytes=64)
+        w2_scales = keep.tile([P, N], U8, name="w2_scales", align_bytes=64)
+        nc.vector.quantize_mx(out=w2_codes[:].bitcast(FP8X4), scales=w2_scales[:], in_=w2_bf[:])
+        for t in ORDER:
+            nc.vector.tensor_tensor(e[t][:], h[t][:].indirect(mb_t[:]), c[t][:], ALU.subtract)
+            nc.scalar.activation(up[t][:], e[t][:], ACT.Relu)
+            nc.scalar.activation(dn0[t][:], e[t][:], ACT.Relu, scale=-1.0)
+            nc.scalar.activation(dn[t][:], dn0[t][:], ACT.Copy, scale=-1.0)
+
+        z = keep.tile([P, S * PACK], BF16, name="z", align_bytes=64)
+        zv = z[:].rearrange("p (s t) -> p s t", t=PACK)
+
+        def put_max(t):
+            h3[t] = ring.tile([P, S], F32, name="h3")
+            nc.vector.tensor_tensor(h3[t][:].indirect(ma_t[:]), c[t][:], up[t][:], ALU.add)
+
+        def put_min(t):
+            nc.vector.tensor_tensor(h3[t][:].indirect(mb_t[:]), c[t][:], dn[t][:], ALU.add)
+            if t != ORDER[-1]:
+                nc.scalar.activation(zv[:, :, t], h3[t][:], ACT.Copy, scale=gain[:, t : t + 1])
+
+        put_max(ORDER[0])
+        for n in range(1, PACK):
+            put_max(ORDER[n])
+            put_min(ORDER[n - 1])
+        last = ORDER[-1]
+        put_min(last)
+        for half in range(2):
+            cols = slice(half * HALF, (half + 1) * HALF)
+            nc.vector.tensor_scalar(zv[:, cols, last], h3[last][:, cols], gain[:, last : last + 1], None, ALU.mult)
+
+        z_codes = keep.tile([P, S], U32, name="z_codes", align_bytes=64)
+        z_scales = keep.tile([P, S], U8, name="z_scales", align_bytes=64)
+        for half in range(2):
+            cols = slice(half * HALF, (half + 1) * HALF)
+            nc.vector.quantize_mx(out=z_codes[:, cols].bitcast(FP8X4), scales=z_scales[:, cols], in_=z[:, half * HALF * PACK : (half + 1) * HALF * PACK])
+        for half in range(2):
+            cols = slice(half * HALF, (half + 1) * HALF)
+            for mt in range(4):
+                rows = slice(mt * P, (mt + 1) * P)
+                acc = psum.tile([P, S], F32, name="acc")
+                nc.tensor.matmul_mx(
+                    out=acc[:, :HALF],
+                    lhsT=w2_codes[:, rows].bitcast(FP8X4),
+                    lhsT_scale=w2_scales[:, rows],
+                    rhs=z_codes[:, cols].bitcast(FP8X4),
+                    rhs_scale=z_scales[:, cols],
+                    start=True,
+                    stop=True,
+                )
+                res = keep.tile([P, HALF], F32, name=f"res{half}{mt}")
+                if mt % 2 == 0:
+                    nc.scalar.copy(res[:], acc[:, :HALF])
+                else:
+                    nc.vector.tensor_copy(res[:], acc[:, :HALF])
+                nc.sync.dma_start(out=out[rows, cols], in_=res[:])

@@ -37,20 +37,20 @@ def tile_picked_gossip2_none_p_kernel(tc, x_words, x_scales, w1, gn, w2, offs, l
 
         xs_all = keep.tile([P, T], U8, name="xs_all")
         nc.gpsimd.memset(xs_all[:].bitcast(I32), 0)
-        for q in range(4):
-            nc.scalar.dma_start(out=xs_all[32 * q : 32 * q + 4, :].bitcast(I32), in_=x_scales[0][4 * q : 4 * q + 4, :].bitcast(I32))
 
-        for list_tile, src_list in ((offs_t, offs), (la_t, la), (lb_t, lb), (ma_t, ma)):
-            nc.sync.dma_start(out=list_tile[:], in_=src_list)
+        nc.sync.dma_start(out=offs_t[:], in_=offs)
         xw_all = keep.tile([P, T], U32, name="xw_all")
         nc.sync.dma_start(out=xw_all[:].bitcast(I32), in_=x_words[0].rearrange("p n t -> p (n t)").bitcast(I32))
+        for q in range(4):
+            nc.sync.dma_start(out=xs_all[32 * q : 32 * q + 4, :].bitcast(I32), in_=x_scales[0][4 * q : 4 * q + 4, :].bitcast(I32))
         w1_rows = w1.rearrange("(p j) c -> p j c", j=PACK)
         w1_raw = []
         for half, tag in enumerate(("w1_raw", "w_raw")):
             raw = keep.tile([P, PACK, H // 2], F32, name=tag)
             nc.sync.dma_start(out=raw[:], in_=w1_rows[:, :, half * (H // 2) : (half + 1) * (H // 2)])
             w1_raw.append(raw[:].rearrange("p j (m t) -> p m j t", t=PACK))
-        nc.sync.dma_start(out=mb_t[:], in_=mb)
+        for list_tile, src_list in ((la_t, la), (lb_t, lb), (ma_t, ma), (mb_t, mb)):
+            nc.sync.dma_start(out=list_tile[:], in_=src_list)
 
         xw = keep.tile([P, S], U32, name="xw", align_bytes=64)
         nc.vector.tensor_copy(xw[:], xw_all[:].indirect(offs_t[:]))
@@ -141,9 +141,8 @@ def tile_picked_gossip2_none_p_kernel(tc, x_words, x_scales, w1, gn, w2, offs, l
             put_min(ORDER[n - 1])
         last = ORDER[-1]
         put_min(last)
-        for half in range(2):
-            cols = slice(half * HALF, (half + 1) * HALF)
-            nc.vector.tensor_scalar(zv[:, cols, last], h3[last][:, cols], gain[:, last : last + 1], None, ALU.mult)
+        nc.vector.tensor_scalar(zv[:, :HALF, last], h3[last][:, :HALF], gain[:, last : last + 1], None, ALU.mult)
+        nc.scalar.activation(zv[:, HALF:, last], h3[last][:, HALF:], ACT.Copy, scale=gain[:, last : last + 1])
 
         z_codes = keep.tile([P, S], U32, name="z_codes", align_bytes=64)
         z_scales = keep.tile([P, S], U8, name="z_scales", align_bytes=64)

from contextlib import ExitStack

import concourse.mybir as mybir

K, T, S, V, N, H = 512, 2048, 512, 256, 512, 512
FLOPS = 2 * K * H * S + 2 * H * N * S

F32 = mybir.dt.float32
BF16 = mybir.dt.bfloat16
I32 = mybir.dt.int32
U32 = mybir.dt.uint32
U16 = mybir.dt.uint16
U8 = mybir.dt.uint8
FP8X4 = mybir.dt.float8_e4m3fn_x4
ALU = mybir.AluOpType
ACT = mybir.ActivationFunctionType

P = 128
PACK = 4
HALF = S // 2
W1_SPLIT = 40
ORDER = (0, 2, 3, 1)


def tile_picked_gossip2_none_p_kernel(tc, x_words, x_scales, w1, gn, w2, offs, la, lb, ma, mb, out):
    nc = tc.nc
    with ExitStack() as ctx:
        keep = ctx.enter_context(tc.tile_pool(name="keep", bufs=1))
        ring = ctx.enter_context(tc.tile_pool(name="ring", bufs=3))
        psum = ctx.enter_context(tc.psum_pool(name="psum", bufs=8))

        offs_t = keep.tile([P, S // 16], U16, name="offs_t")
        la_t = keep.tile([P, V // 16], U16, name="la_t")
        lb_t = keep.tile([P, V // 16], U16, name="lb_t")
        ma_t = keep.tile([P, V // 16], U16, name="ma_t")
        mb_t = keep.tile([P, V // 16], U16, name="mb_t")

        xs_all = keep.tile([P, T], U8, name="xs_all")
        nc.gpsimd.memset(xs_all[:].bitcast(I32), 0)

        nc.sync.dma_start(out=offs_t[:], in_=offs)
        xw_all = keep.tile([P, T], U32, name="xw_all")
        nc.sync.dma_start(out=xw_all[:].bitcast(I32), in_=x_words[0].rearrange("p n t -> p (n t)").bitcast(I32))
        for q in range(4):
            nc.sync.dma_start(out=xs_all[32 * q : 32 * q + 4, :].bitcast(I32), in_=x_scales[0][4 * q : 4 * q + 4, :].bitcast(I32))
        w1_rows = w1.rearrange("(p j) c -> p j c", j=PACK)
        w1_raw = []
        for half, tag in enumerate(("w1_raw", "w_raw")):
            raw = keep.tile([P, PACK, H // 2], F32, name=tag)
            nc.sync.dma_start(out=raw[:], in_=w1_rows[:, :, half * (H // 2) : (half + 1) * (H // 2)])
            w1_raw.append(raw[:].rearrange("p j (m t) -> p m j t", t=PACK))
        for list_tile, src_list in ((la_t, la), (lb_t, lb), (ma_t, ma), (mb_t, mb)):
            nc.sync.dma_start(out=list_tile[:], in_=src_list)

        xw = keep.tile([P, S], U32, name="xw", align_bytes=64)
        nc.vector.tensor_copy(xw[:], xw_all[:].indirect(offs_t[:]))
        xs = keep.tile([P, S], U8, name="xs", align_bytes=64)
        nc.vector.tensor_copy(xs[:], xs_all[:].indirect(offs_t[:]))

        w1_bf = keep.tile([P, PACK * H], BF16, name="w1_bf", align_bytes=64)
        dst = w1_bf[:].rearrange("p (t m j) -> p m j t", t=PACK, j=PACK)
        nc.scalar.copy(dst[:, :64], w1_raw[0])
        nc.vector.tensor_copy(dst[:, 64 : 64 + W1_SPLIT], w1_raw[1][:, :W1_SPLIT])
        nc.scalar.copy(dst[:, 64 + W1_SPLIT :], w1_raw[1][:, W1_SPLIT:])
        w1_codes = keep.tile([P, H], U32, name="w1_codes", align_bytes=64)
        w1_scales = keep.tile([P, H], U8, name="w1_scales", align_bytes=64)
        for c0, c1 in ((0, P), (2 * P, 4 * P), (P, 2 * P)):
            nc.vector.quantize_mx(out=w1_codes[:, c0:c1].bitcast(FP8X4), scales=w1_scales[:, c0:c1], in_=w1_bf[:, PACK * c0 : PACK * c1])

        w2_raw = keep.tile([P, PACK, N], F32, name="w_raw")
        nc.sync.dma_start(out=w2_raw[:], in_=w2.rearrange("(p j) c -> p j c", j=PACK))

        gain = keep.tile([P, PACK], F32, name="xs_all")
        nc.sync.dma_start(out=gain[:], in_=gn.rearrange("(p t) o -> p (t o)", t=PACK))
        y = [keep.tile([P, S], F32, name=f"y{t}") for t in range(PACK)]
        for t in ORDER:
            cols = slice(t * P, (t + 1) * P)
            for c0, c1 in ((0, HALF), (HALF, S)) if t == 0 else ((0, S),):
                acc = psum.tile([P, S], F32, name="acc")
                nc.tensor.matmul_mx(
                    out=acc[:, : c1 - c0],
                    lhsT=w1_codes[:, cols].bitcast(FP8X4),
                    lhsT_scale=w1_scales[:, cols],
                    rhs=xw[:, c0:c1].bitcast(FP8X4),
                    rhs_scale=xs[:, c0:c1],
                    start=True,
                    stop=True,
                )
                nc.scalar.activation(y[t][:, c0:c1], acc[:, : c1 - c0], ACT.Copy, scale=0.5)

        def small(name):
            return [keep.tile([P, V], F32, name=f"{name}{t}") for t in range(PACK)]

        a, b, a2, b2 = small("a"), small("b"), small("a2"), small("b2")
        c, e, up, dn0, dn = small("c"), small("e"), small("up"), small("dn0"), small("dn")
        h = [keep.tile([P, S], F32, name=f"h{t}") for t in range(PACK)]
        h3 = {}

        for t in ORDER:
            nc.vector.tensor_copy(a[t][:], y[t][:].indirect(la_t[:]))
            nc.vector.tensor_copy(b[t][:], y[t][:].indirect(lb_t[:]))
            nc.scalar.activation(a2[t][:], a[t][:], ACT.Copy, scale=-0.5)
            nc.scalar.activation(b2[t][:], b[t][:], ACT.Copy, scale=1.5)
        for t in ORDER:
            nc.vector.tensor_tensor(h[t][:].indirect(la_t[:]), a[t][:], b[t][:], ALU.add)

        w2_bf = keep.tile([P, PACK * N], BF16, name="w2_bf", align_bytes=64)
        dst2 = w2_bf[:].rearrange("p (c i j) -> p c j i", i=4, j=PACK)
        src2 = w2_raw[:].rearrange("p j (c i) -> p c j i", i=4)
        for mt in range(4):
            nc.scalar.copy(dst2[:, 32 * mt : 32 * (mt + 1)], src2[:, 32 * mt : 32 * (mt + 1)])

        for t in ORDER:
            nc.vector.tensor_tensor(h[t][:].indirect(lb_t[:]), a2[t][:], b2[t][:], ALU.add)
        for t in ORDER:
            nc.vector.tensor_copy(c[t][:], h[t][:].indirect(ma_t[:]))
        w2_codes = keep.tile([P, N], U32, name="w2_codes", align_bytes=64)
        w2_scales = keep.tile([P, N], U8, name="w2_scales", align_bytes=64)
        nc.vector.quantize_mx(out=w2_codes[:].bitcast(FP8X4), scales=w2_scales[:], in_=w2_bf[:])
        for t in ORDER:
            nc.vector.tensor_tensor(e[t][:], h[t][:].indirect(mb_t[:]), c[t][:], ALU.subtract)
            nc.scalar.activation(up[t][:], e[t][:], ACT.Relu)
            nc.scalar.activation(dn0[t][:], e[t][:], ACT.Relu, scale=-1.0)
            nc.scalar.activation(dn[t][:], dn0[t][:], ACT.Copy, scale=-1.0)

        z = keep.tile([P, S * PACK], BF16, name="z", align_bytes=64)
        zv = z[:].rearrange("p (s t) -> p s t", t=PACK)

        def put_max(t):
            h3[t] = ring.tile([P, S], F32, name="h3")
            nc.vector.tensor_tensor(h3[t][:].indirect(ma_t[:]), c[t][:], up[t][:], ALU.add)

        def put_min(t):
            nc.vector.tensor_tensor(h3[t][:].indirect(mb_t[:]), c[t][:], dn[t][:], ALU.add)
            if t != ORDER[-1]:
                nc.scalar.activation(zv[:, :, t], h3[t][:], ACT.Copy, scale=gain[:, t : t + 1])

        put_max(ORDER[0])
        for n in range(1, PACK):
            put_max(ORDER[n])
            put_min(ORDER[n - 1])
        last = ORDER[-1]
        put_min(last)
        nc.vector.tensor_scalar(zv[:, :HALF, last], h3[last][:, :HALF], gain[:, last : last + 1], None, ALU.mult)
        nc.scalar.activation(zv[:, HALF:, last], h3[last][:, HALF:], ACT.Copy, scale=gain[:, last : last + 1])

        z_codes = keep.tile([P, S], U32, name="z_codes", align_bytes=64)
        z_scales = keep.tile([P, S], U8, name="z_scales", align_bytes=64)
        for half in range(2):
            cols = slice(half * HALF, (half + 1) * HALF)
            nc.vector.quantize_mx(out=z_codes[:, cols].bitcast(FP8X4), scales=z_scales[:, cols], in_=z[:, half * HALF * PACK : (half + 1) * HALF * PACK])
        for half in range(2):
            cols = slice(half * HALF, (half + 1) * HALF)
            for mt in range(4):
                rows = slice(mt * P, (mt + 1) * P)
                acc = psum.tile([P, S], F32, name="acc")
                nc.tensor.matmul_mx(
                    out=acc[:, :HALF],
                    lhsT=w2_codes[:, rows].bitcast(FP8X4),
                    lhsT_scale=w2_scales[:, rows],
                    rhs=z_codes[:, cols].bitcast(FP8X4),
                    rhs_scale=z_scales[:, cols],
                    start=True,
                    stop=True,
                )
                res = keep.tile([P, HALF], F32, name=f"res{half}{mt}")
                if mt % 2 == 0:
                    nc.scalar.copy(res[:], acc[:, :HALF])
                else:
                    nc.vector.tensor_copy(res[:], acc[:, :HALF])
                nc.sync.dma_start(out=out[rows, cols], in_=res[:])
